import numpy as np
import ml_dtypes


def mxq(x, axis, fmt="e4m3"):
    dtype, down = {"e4m3": (ml_dtypes.float8_e4m3fn, 7), "e5m2": (ml_dtypes.float8_e5m2, 14)}[fmt]
    v = np.moveaxis(np.asarray(x, np.float32).astype(ml_dtypes.bfloat16).astype(np.float64), axis, -1)
    blocks = v.reshape(v.shape[:-1] + (-1, 32))
    amax = np.abs(blocks).max(-1, keepdims=True)
    byte = np.maximum(np.where(amax > 0, np.frexp(amax)[1] - 1 + 127, 0) - down, 1)
    scale = np.exp2(byte - 127.0)
    codes = (blocks / scale).astype(np.float32).astype(dtype).astype(np.float64)
    return np.moveaxis((codes * scale).reshape(v.shape), -1, axis)


WIDE = False


def mx_kscale(k):
    if not WIDE:
        return np.ones(k)
    levels = np.array([10, -10, 5, -5, 0])
    if k % 512:
        return np.exp2(np.random.permutation(np.resize(levels, k // 32))).repeat(32)
    a = np.empty((k // 512, 16))
    for p in range(k // 512):
        a[p, :8] = np.random.permutation(np.resize(levels, 8))
        for g in range(8):
            far = levels[np.abs(levels - a[p, g]) >= 10]
            a[p, g + 8] = far[np.random.randint(len(far))]
    return np.exp2(a.ravel()).repeat(32)


BF16 = ml_dtypes.bfloat16


def bf(x):
    return np.asarray(x, np.float32).astype(BF16)


def f64(x):
    return np.asarray(x).astype(np.float64)


V, M, C, P = 2048, 512, 512, 2


def heat_decay(s, lam, t):
    return s * np.exp(-lam[:, None] * t[None, :])


def complex_map(z, ar, aim):
    zq = mxq(z, 2, "e4m3")
    r = zq @ mxq(ar, 0, "e4m3")
    q = zq @ mxq(aim, 0, "e4m3")
    er = r[0] - q[1]
    ei = r[1] + q[0]
    return er, ei


def draw0():
    u, w = mx_kscale(M), mx_kscale(C)
    return {
        "s": bf(np.random.standard_normal((M, C)) * u[:, None]),
        "lam": bf(np.random.uniform(0.0, 4.0, M)),
        "t": bf(np.random.uniform(0.2, 1.0, C)),
        "grad": bf(np.random.standard_normal((P, V, M)) * 1.5 / np.sqrt(M) / u),
        "gain": bf((1.0 + 0.1 * np.random.standard_normal(C)) * w),
        "ar": bf(np.random.standard_normal((C, C)) / np.sqrt(C) / w[:, None]),
        "aim": bf(np.random.standard_normal((C, C)) / np.sqrt(C) / w[:, None]),
    }


def core(s, lam, t, grad, gain, ar, aim):
    h = heat_decay(f64(s), f64(lam), f64(t))
    g = mxq(f64(grad), 2, "e4m3") @ mxq(h, 0, "e4m3")
    z = g * f64(gain)[None, None, :]
    er, ei = complex_map(z, f64(ar), f64(aim))
    return np.tanh(g[0] * er + g[1] * ei)


def e4m3fn_bytes(y):
    return np.clip(np.asarray(y, np.float64), -448.0, 448.0).astype(np.float32).astype(ml_dtypes.float8_e4m3fn).view(np.uint8)


def e4m3fn_values(b):
    return np.asarray(b, np.uint8).view(ml_dtypes.float8_e4m3fn).astype(np.float64)


def setup_inputs():
    d = draw0()
    x0 = np.asarray(d['grad']).astype(np.float64)
    s = (np.max(np.abs(x0), axis=(0, 1), keepdims=True) / 448.0).astype(np.float32)
    out = {}
    for k, v in d.items():
        if k == 'grad':
            out['grad_bytes'] = e4m3fn_bytes(x0 / s.astype(np.float64))
            out['grad_scale'] = s
        else:
            out[k] = v
    return out


def reference(s, lam, t, grad_bytes, grad_scale, gain, ar, aim):
    return core(s, lam, t, e4m3fn_values(grad_bytes) * grad_scale.astype(np.float64), gain, ar, aim)

@@ -1,0 +1,285 @@
+from contextlib import ExitStack
+
+import concourse.mybir as mybir
+from concourse.masks import make_identity
+
+V, M, C, P = 2048, 512, 512, 2
+FLOPS = 2 * P * V * M * C + 4 * 2 * V * C * C
+
+F32 = mybir.dt.float32
+BF16 = mybir.dt.bfloat16
+U32 = mybir.dt.uint32
+U8 = mybir.dt.uint8
+FP8 = mybir.dt.float8_e4m3fn
+FP8X4 = mybir.dt.float8_e4m3fn_x4
+ACT = mybir.ActivationFunctionType
+ALU = mybir.AluOpType
+
+NP = 128
+NT = 4
+UNITS = V // NP
+V_CASTS = 3
+
+
+def tile_diffusionnetheatgradient_kernel(tc, s, lam, t, grad_bytes, grad_scale, gain, ar, aim, out):
+    nc = tc.nc
+    with ExitStack() as ctx:
+        keep = ctx.enter_context(tc.tile_pool(name="keep", bufs=1))
+        ring = ctx.enter_context(tc.tile_pool(name="ring", bufs=3))
+        psum = ctx.enter_context(tc.psum_pool(name="psum", bufs=1))
+
+        ident = keep.tile([NP, NP], F32)
+        make_identity(nc, ident[:])
+
+        s_raw = keep.tile([NP, NT, C], BF16)
+        ar_raw = keep.tile([NP, NT, C], BF16)
+        ai_raw = keep.tile([NP, NT, C], BF16)
+        t_row = keep.tile([NP, C], BF16)
+        lam_col = keep.tile([NP, NT], BF16)
+        neg_lam = keep.tile([NP, NT], F32)
+        gain_col = keep.tile([NP, NT], BF16)
+        scale_col = keep.tile([NP, NT], F32)
+        decay = keep.tile([NP, NT, C], F32)
+        warm = keep.tile([NP, 1], F32)
+        warm_out = keep.tile([NP, 1], F32)
+
+        raw = {}
+        chunks = [(0, 1), (1, 1), (2, 2), (4, 4), (8, 4), (12, 4)]
+        by_unit = {}
+
+        def load_chunk(n):
+            first, count = chunks[n]
+            codes = keep.tile([NP, count, P, M], U8, name="bytes%d" % n)
+            for p in range(P):
+                nc.sync.dma_start(
+                    out=codes[:, :, p, :],
+                    in_=grad_bytes[p].rearrange("(q i) k -> q i k", i=UNITS)[:, first : first + count, :],
+                )
+            for i in range(count):
+                by_unit[first + i] = codes[:, i, :, :]
+
+        xb, tb, xg, xc, xs, gb, gs, zg, zc, zs, eb, mm, ob = ({} for _ in range(13))
+        weights = {}
+
+        def cast(i):
+            if not 0 <= i < UNITS:
+                return
+            x_bf = ring.tile([NP, P * M], BF16)
+            codes = by_unit[i].rearrange("q p k -> q (p k)").bitcast(FP8)
+            if i < V_CASTS:
+                nc.vector.tensor_copy(out=x_bf[:], in_=codes)
+            else:
+                nc.scalar.copy(out=x_bf[:], in_=codes)
+            xb[i] = x_bf
+
+        def turn(i):
+            if not 0 <= i < UNITS:
+                return
+            bank = psum.tile([NP, 2, P * NP], F32, name="tb")
+            words = xb[i][:].bitcast(F32)
+            for p in range(P):
+                for u in range(2):
+                    nc.tensor.transpose(
+                        bank[:, u, p * NP : (p + 1) * NP],
+                        words[:, p * 256 + u : (p + 1) * 256 : 2],
+                        ident[:],
+                    )
+            tb[i] = bank
+
+        def scale_x(i):
+            if not 0 <= i < UNITS:
+                return
+            x_grp = ring.tile([NP, P * NP * NT], BF16, align_bytes=64)
+            nc.vector.tensor_tensor(
+                out=x_grp[:].rearrange("k (r u e) -> k r u e", u=2, e=2),
+                in0=tb[i][:].rearrange("k u r -> k (u r)").bitcast(BF16).rearrange("k (u r e) -> k r u e", u=2, e=2),
+                in1=scale_col[:].rearrange("k (u e) -> k u e", u=2).unsqueeze(1).to_broadcast([NP, P * NP, 2, 2]),
+                op=ALU.mult,
+            )
+            xg[i] = x_grp
+
+        def quant(src, codes_name, width):
+            codes = ring.tile([NP, width], U32, align_bytes=64, name=codes_name)
+            scales = ring.tile([NP, width], U8, align_bytes=64, name=codes_name + "_s")
+            nc.vector.quantize_mx(out=codes[:].bitcast(FP8X4), scales=scales[:], in_=src)
+            return codes, scales
+
+        def quant_x(i):
+            if 0 <= i < UNITS:
+                xc[i] = quant(xg[i][:], "xc", P * NP)
+
+        def quant_z(i):
+            if 0 <= i < UNITS:
+                zc[i] = quant(zg[i][:].rearrange("k p n j -> k (p n j)"), "zc", P * NP)
+
+        def mx(dst, w, tt, mov, p, start, stop):
+            wc, ws = weights[w]
+            cols = slice(tt * NP, (tt + 1) * NP)
+            rows = slice(p * NP, (p + 1) * NP)
+            nc.tensor.matmul_mx(
+                out=dst,
+                lhsT=wc[:, cols].bitcast(FP8X4),
+                lhsT_scale=ws[:, cols],
+                rhs=mov[0][:, rows].bitcast(FP8X4),
+                rhs_scale=mov[1][:, rows],
+                start=start,
+                stop=stop,
+            )
+
+        def stage1(i):
+            if not 0 <= i < UNITS:
+                return
+            for p in range(P):
+                bank = psum.tile([NP, NT, NP], F32, name="gb%d" % p, bufs=2)
+                for tt in range(NT):
+                    mx(bank[:, tt, :], "h", tt, xc[i], p, True, True)
+                gb[i, p] = bank
+
+        def g_out(i, p):
+            if not 0 <= i < UNITS:
+                return
+            g_sb = ring.tile([NP, NT, NP], F32, name="gs%d" % p, bufs=4)
+            nc.scalar.copy(out=g_sb[:], in_=gb[i, p][:])
+            gs[i, p] = g_sb
+
+        def gain_z(i, p):
+            if not 0 <= i < UNITS:
+                return
+            if p == 0:
+                z_grp = keep.tile([NP, P, NP, NT], BF16, align_bytes=64)
+                zg[i] = z_grp
+            eng, g_in = (nc.vector, gb[i, p]) if p == 0 else (nc.gpsimd, gs[i, p])
+            eng.tensor_tensor(
+                out=zg[i][:, p, :, :],
+                in0=g_in[:].rearrange("c j n -> c n j"),
+                in1=gain_col[:].unsqueeze(1).to_broadcast([NP, NP, NT]),
+                op=ALU.mult,
+            )
+
+        def stage2(i):
+            if not 0 <= i < UNITS:
+                return
+            for part, w0, w1 in ((0, "ar", "nai"), (1, "ai", "ar")):
+                if i == UNITS - 1:
+                    bank = psum.tile([NP, NT, NP], F32, name="gb%d" % part, bufs=2)
+                else:
+                    bank = psum.tile([NP, NT, NP], F32, name="eb%d" % part)
+                for tt in range(NT):
+                    mx(bank[:, tt, :], w0, tt, zc[i], 0, True, False)
+                    mx(bank[:, tt, :], w1, tt, zc[i], 1, False, True)
+                eb[i, part] = bank
+
+        def product(i, part):
+            if not 0 <= i < UNITS:
+                return
+            prod = ring.tile([NP, NT, NP], F32, name="mm%d" % part)
+            nc.vector.tensor_tensor(out=prod[:], in0=eb[i, part][:], in1=gs[i, part][:], op=ALU.mult)
+            mm[i, part] = prod
+
+        def turn_back(i):
+            if not 0 <= i < UNITS:
+                return
+            bank = psum.tile([NP, NT, NP], F32, name="ob")
+            for tt in range(NT):
+                for part in range(2):
+                    nc.tensor.matmul(
+                        out=bank[:, tt, :],
+                        lhsT=mm[i, part][:, tt, :],
+                        rhs=ident[:],
+                        is_transpose=True,
+                        start=(part == 0),
+                        stop=(part == 1),
+                    )
+            ob[i] = bank
+
+        def finish(i):
+            if not 0 <= i < UNITS:
+                return
+            o_sb = ring.tile([NP, C], F32, name="os")
+            nc.scalar.activation(
+                out=o_sb[:].rearrange("v (c j) -> v c j", j=NT),
+                in_=ob[i][:].rearrange("v j c -> v c j"),
+                func=ACT.Tanh,
+            )
+            nc.sync.dma_start(out=out.rearrange("(q i) c -> q i c", i=UNITS)[:, i, :], in_=o_sb[:])
+
+        def quant_weight(name, src):
+            codes = keep.tile([NP, C], U32, align_bytes=64, name=name + "_c")
+            scales = keep.tile([NP, C], U8, align_bytes=64, name=name + "_s")
+            nc.vector.quantize_mx(out=codes[:].bitcast(FP8X4), scales=scales[:], in_=src)
+            weights[name] = (codes, scales)
+
+        with tc.manual_schedule():
+            nc.sync.dma_start(out=s_raw[:], in_=s.rearrange("(p j) c -> p j c", j=NT))
+            nc.scalar.dma_start(out=t_row[:], in_=t.partition_broadcast(NP))
+            nc.scalar.dma_start(out=lam_col[:], in_=lam.rearrange("(p j) -> p j", j=NT))
+            nc.scalar.dma_start(out=scale_col[:], in_=grad_scale.rearrange("a b (p j) -> p (a b j)", j=NT))
+            nc.scalar.dma_start(out=gain_col[:], in_=gain.rearrange("(p j) -> p j", j=NT))
+            load_chunk(0)
+            load_chunk(1)
+            nc.sync.dma_start(out=ar_raw[:], in_=ar.rearrange("(p j) c -> p j c", j=NT))
+            nc.sync.dma_start(out=ai_raw[:], in_=aim.rearrange("(p j) c -> p j c", j=NT))
+            for n in range(2, len(chunks)):
+                load_chunk(n)
+
+            nc.vector.memset(warm[:], 0.0)
+            nc.scalar.activation(out=warm_out[:], in_=warm[:], func=ACT.Exp)
+            nc.vector.tensor_scalar(out=neg_lam[:], in0=lam_col[:], scalar1=-1.0, scalar2=None, op0=ALU.mult)
+            for j in range(NT):
+                nc.scalar.activation(out=decay[:, j, :], in_=t_row[:], func=ACT.Exp, scale=neg_lam[:, j : j + 1])
+
+            h_grp = keep.tile([NP, NT * C], BF16, align_bytes=64)
+            ar_grp = keep.tile([NP, NT * C], BF16, align_bytes=64)
+            ai_grp = keep.tile([NP, NT * C], BF16, align_bytes=64)
+            nai_grp = keep.tile([NP, NT * C], BF16, align_bytes=64)
+
+            def grouped(tile):
+                return tile[:].rearrange("p (t m j) -> p t m j", t=NT, j=NT)
+
+            def permuted(tile):
+                return tile[:].rearrange("p j (m t) -> p t m j", t=NT)
+
+            def prepare(name, raw_tile, grp, engine):
+                for tt in range(NT):
+                    piece = grouped(grp)[:, tt, :, :]
+                    source = permuted(raw_tile)[:, tt, :, :]
+                    if engine == "scalar":
+                        nc.scalar.activation(out=piece, in_=source, func=ACT.Copy, scale=-1.0)
+                    else:
+                        nc.gpsimd.tensor_scalar(out=piece, in0=source, scalar1=1.0, scalar2=0.0, op0=ALU.mult, op1=ALU.add)
+
+            prepare("ar", ar_raw, ar_grp, "gpsimd")
+            prepare("ai", ai_raw, ai_grp, "gpsimd")
+            for step in range(-5, UNITS):
+                scale_x(step + 3)
+                if step == -3:
+                    nc.vector.tensor_tensor(out=grouped(h_grp), in0=permuted(decay), in1=permuted(s_raw), op=ALU.mult)
+                turn(step + 4)
+                cast(step + 5)
+                g_out(step + 2, 0)
+                g_out(step + 2, 1)
+                late = step + 1 == UNITS - 1
+                if not late:
+                    for part in range(2):
+                        product(step, part)
+                for p in range(P):
+                    gain_z(step + 1, p)
+                if late:
+                    quant_z(step + 1)
+                    for part in range(2):
+                        product(step, part)
+                    stage2(step + 1)
+                turn_back(step)
+                finish(step)
+                if step == -3:
+                    prepare("nai", ai_raw, nai_grp, "scalar")
+                    quant_weight("h", h_grp[:])
+                if step == -1:
+                    quant_weight("ar", ar_grp[:])
+                    quant_weight("nai", nai_grp[:])
+                    quant_weight("ai", ai_grp[:])
+                quant_x(step + 3)
+                if not late:
+                    quant_z(step + 1)
+                    stage2(step + 1)
+                stage1(step + 3)

@@ -19,6 +19,7 @@ NP = 128
 NT = 4
 UNITS = V // NP
 V_CASTS = 3
+G_HALVES = ()
 
 
 def tile_diffusionnetheatgradient_kernel(tc, s, lam, t, grad_bytes, grad_scale, gain, ar, aim, out):
@@ -50,11 +51,12 @@ def tile_diffusionnetheatgradient_kernel(tc, s, lam, t, grad_bytes, grad_scale, 
         def load_chunk(n):
             first, count = chunks[n]
             codes = keep.tile([NP, count, P, M], U8, name="bytes%d" % n)
-            for p in range(P):
-                nc.sync.dma_start(
-                    out=codes[:, :, p, :],
-                    in_=grad_bytes[p].rearrange("(q i) k -> q i k", i=UNITS)[:, first : first + count, :],
-                )
+            view = grad_bytes.rearrange("p (q i) k -> q i p k", i=UNITS)
+            if count == 1:
+                nc.sync.dma_start(out=codes[:, 0, :, :], in_=view[:, first, :, :])
+            else:
+                for p in range(P):
+                    nc.sync.dma_start(out=codes[:, :, p, :], in_=view[:, first : first + count, p, :])
             for i in range(count):
                 by_unit[first + i] = codes[:, i, :, :]
 
@@ -148,7 +150,7 @@ def tile_diffusionnetheatgradient_kernel(tc, s, lam, t, grad_bytes, grad_scale, 
             if p == 0:
                 z_grp = keep.tile([NP, P, NP, NT], BF16, align_bytes=64)
                 zg[i] = z_grp
-            eng, g_in = (nc.vector, gb[i, p]) if p == 0 else (nc.gpsimd, gs[i, p])
+            eng, g_in = (nc.vector, gb[i, p]) if p not in G_HALVES else (nc.gpsimd, gs[i, p])
             eng.tensor_tensor(
                 out=zg[i][:, p, :, :],
                 in0=g_in[:].rearrange("c j n -> c n j"),
@@ -210,12 +212,12 @@ def tile_diffusionnetheatgradient_kernel(tc, s, lam, t, grad_bytes, grad_scale, 
             weights[name] = (codes, scales)
 
         with tc.manual_schedule():
+            load_chunk(0)
             nc.sync.dma_start(out=s_raw[:], in_=s.rearrange("(p j) c -> p j c", j=NT))
             nc.scalar.dma_start(out=t_row[:], in_=t.partition_broadcast(NP))
             nc.scalar.dma_start(out=lam_col[:], in_=lam.rearrange("(p j) -> p j", j=NT))
             nc.scalar.dma_start(out=scale_col[:], in_=grad_scale.rearrange("a b (p j) -> p (a b j)", j=NT))
             nc.scalar.dma_start(out=gain_col[:], in_=gain.rearrange("(p j) -> p j", j=NT))
-            load_chunk(0)
             load_chunk(1)
             nc.sync.dma_start(out=ar_raw[:], in_=ar.rearrange("(p j) c -> p j c", j=NT))
             nc.sync.dma_start(out=ai_raw[:], in_=aim.rearrange("(p j) c -> p j c", j=NT))

@@ -19,7 +19,8 @@ NP = 128
 NT = 4
 UNITS = V // NP
 V_CASTS = 3
-G_HALVES = ()
+V_COLS = (128, 0)
+W = P * NP * NT
 
 
 def tile_diffusionnetheatgradient_kernel(tc, s, lam, t, grad_bytes, grad_scale, gain, ar, aim, out):
@@ -35,7 +36,8 @@ def tile_diffusionnetheatgradient_kernel(tc, s, lam, t, grad_bytes, grad_scale, 
         s_raw = keep.tile([NP, NT, C], BF16)
         ar_raw = keep.tile([NP, NT, C], BF16)
         ai_raw = keep.tile([NP, NT, C], BF16)
-        t_row = keep.tile([NP, C], BF16)
+        t_rows = keep.tile([NP, C], BF16)
+        ones = keep.tile([NP, NP], BF16)
         lam_col = keep.tile([NP, NT], BF16)
         neg_lam = keep.tile([NP, NT], F32)
         gain_col = keep.tile([NP, NT], BF16)
@@ -52,15 +54,12 @@ def tile_diffusionnetheatgradient_kernel(tc, s, lam, t, grad_bytes, grad_scale, 
             first, count = chunks[n]
             codes = keep.tile([NP, count, P, M], U8, name="bytes%d" % n)
             view = grad_bytes.rearrange("p (q i) k -> q i p k", i=UNITS)
-            if count == 1:
-                nc.sync.dma_start(out=codes[:, 0, :, :], in_=view[:, first, :, :])
-            else:
-                for p in range(P):
-                    nc.sync.dma_start(out=codes[:, :, p, :], in_=view[:, first : first + count, p, :])
+            for i in range(count):
+                nc.sync.dma_start(out=codes[:, i, :, :], in_=view[:, first + i, :, :])
             for i in range(count):
                 by_unit[first + i] = codes[:, i, :, :]
 
-        xb, tb, xg, xc, xs, gb, gs, zg, zc, zs, eb, mm, ob = ({} for _ in range(13))
+        xb, tb, xc, gb, gs, zc, eb, mm, ob, pairs = {}, {}, {}, {}, {}, {}, {}, {}, {}, {}
         weights = {}
 
         def cast(i):
@@ -91,33 +90,40 @@ def tile_diffusionnetheatgradient_kernel(tc, s, lam, t, grad_bytes, grad_scale, 
         def scale_x(i):
             if not 0 <= i < UNITS:
                 return
-            x_grp = ring.tile([NP, P * NP * NT], BF16, align_bytes=64)
             nc.vector.tensor_tensor(
-                out=x_grp[:].rearrange("k (r u e) -> k r u e", u=2, e=2),
+                out=pair_tile(i - 2)[:, 0:W].rearrange("k (r u e) -> k r u e", u=2, e=2),
                 in0=tb[i][:].rearrange("k u r -> k (u r)").bitcast(BF16).rearrange("k (u r e) -> k r u e", u=2, e=2),
                 in1=scale_col[:].rearrange("k (u e) -> k u e", u=2).unsqueeze(1).to_broadcast([NP, P * NP, 2, 2]),
                 op=ALU.mult,
             )
-            xg[i] = x_grp
 
-        def quant(src, codes_name, width):
-            codes = ring.tile([NP, width], U32, align_bytes=64, name=codes_name)
-            scales = ring.tile([NP, width], U8, align_bytes=64, name=codes_name + "_s")
-            nc.vector.quantize_mx(out=codes[:].bitcast(FP8X4), scales=scales[:], in_=src)
-            return codes, scales
+        def pair_tile(n):
+            if n not in pairs:
+                pair = keep.tile([NP, 2 * W], BF16, align_bytes=64)
+                pairs[n] = pair
+            return pairs[n]
 
-        def quant_x(i):
-            if 0 <= i < UNITS:
-                xc[i] = quant(xg[i][:], "xc", P * NP)
-
-        def quant_z(i):
-            if 0 <= i < UNITS:
-                zc[i] = quant(zg[i][:].rearrange("k p n j -> k (p n j)"), "zc", P * NP)
+        def quant(n):
+            has_x, has_z = 0 <= n + 2 < UNITS, 0 <= n < UNITS
+            if not (has_x or has_z):
+                return
+            lo, hi = (0 if has_x else W), (2 * W if has_z else W)
+            codes = ring.tile([NP, 2 * W // NT], U32, align_bytes=64)
+            scales = ring.tile([NP, 2 * W // NT], U8, align_bytes=64)
+            nc.vector.quantize_mx(
+                out=codes[:, lo // NT : hi // NT].bitcast(FP8X4),
+                scales=scales[:, lo // NT : hi // NT],
+                in_=pairs[n][:, lo:hi],
+            )
+            if has_x:
+                xc[n + 2] = (codes, scales, 0)
+            if has_z:
+                zc[n] = (codes, scales, W // NT)
 
         def mx(dst, w, tt, mov, p, start, stop):
             wc, ws = weights[w]
             cols = slice(tt * NP, (tt + 1) * NP)
-            rows = slice(p * NP, (p + 1) * NP)
+            rows = slice(mov[2] + p * NP, mov[2] + (p + 1) * NP)
             nc.tensor.matmul_mx(
                 out=dst,
                 lhsT=wc[:, cols].bitcast(FP8X4),
@@ -131,8 +137,8 @@ def tile_diffusionnetheatgradient_kernel(tc, s, lam, t, grad_bytes, grad_scale, 
         def stage1(i):
             if not 0 <= i < UNITS:
                 return
-            for p in range(P):
-                bank = psum.tile([NP, NT, NP], F32, name="gb%d" % p, bufs=2)
+            for p in (1, 0):
+                bank = psum.tile([NP, NT, NP], F32, name="gb%d" % p)
                 for tt in range(NT):
                     mx(bank[:, tt, :], "h", tt, xc[i], p, True, True)
                 gb[i, p] = bank
@@ -144,28 +150,28 @@ def tile_diffusionnetheatgradient_kernel(tc, s, lam, t, grad_bytes, grad_scale, 
             nc.scalar.copy(out=g_sb[:], in_=gb[i, p][:])
             gs[i, p] = g_sb
 
-        def gain_z(i, p):
+        def gain_z(i, p, eng):
             if not 0 <= i < UNITS:
                 return
-            if p == 0:
-                z_grp = keep.tile([NP, P, NP, NT], BF16, align_bytes=64)
-                zg[i] = z_grp
-            eng, g_in = (nc.vector, gb[i, p]) if p not in G_HALVES else (nc.gpsimd, gs[i, p])
-            eng.tensor_tensor(
-                out=zg[i][:, p, :, :],
-                in0=g_in[:].rearrange("c j n -> c n j"),
-                in1=gain_col[:].unsqueeze(1).to_broadcast([NP, NP, NT]),
-                op=ALU.mult,
-            )
+            cut = NP if i == UNITS - 1 else V_COLS[p]
+            lo, hi, g_in = (0, cut, gb[i, p]) if eng is nc.vector else (cut, NP, gs.get((i, p)))
+            if lo < hi:
+                start = W + p * W // 2
+                eng.tensor_tensor(
+                    out=pair_tile(i)[:, start + lo * NT : start + hi * NT].rearrange("c (n j) -> c n j", j=NT),
+                    in0=g_in[:, :, lo:hi].rearrange("c j n -> c n j"),
+                    in1=gain_col[:].unsqueeze(1).to_broadcast([NP, hi - lo, NT]),
+                    op=ALU.mult,
+                )
 
         def stage2(i):
             if not 0 <= i < UNITS:
                 return
             for part, w0, w1 in ((0, "ar", "nai"), (1, "ai", "ar")):
                 if i == UNITS - 1:
-                    bank = psum.tile([NP, NT, NP], F32, name="gb%d" % part, bufs=2)
+                    bank = psum.tile([NP, NT, NP], F32, name="gb%d" % part)
                 else:
-                    bank = psum.tile([NP, NT, NP], F32, name="eb%d" % part)
+                    bank = psum.tile([NP, NT, NP], F32, name="eb%d" % part, bufs=2)
                 for tt in range(NT):
                     mx(bank[:, tt, :], w0, tt, zc[i], 0, True, False)
                     mx(bank[:, tt, :], w1, tt, zc[i], 1, False, True)
@@ -174,14 +180,14 @@ def tile_diffusionnetheatgradient_kernel(tc, s, lam, t, grad_bytes, grad_scale, 
         def product(i, part):
             if not 0 <= i < UNITS:
                 return
-            prod = ring.tile([NP, NT, NP], F32, name="mm%d" % part)
+            prod = ring.tile([NP, NT, NP], F32, name="mm%d" % part, bufs=4)
             nc.vector.tensor_tensor(out=prod[:], in0=eb[i, part][:], in1=gs[i, part][:], op=ALU.mult)
             mm[i, part] = prod
 
         def turn_back(i):
             if not 0 <= i < UNITS:
                 return
-            bank = psum.tile([NP, NT, NP], F32, name="ob")
+            bank = psum.tile([NP, NT, NP], F32, name="tb" if i in (UNITS - 4, UNITS - 2) else "ob")
             for tt in range(NT):
                 for part in range(2):
                     nc.tensor.matmul(
@@ -197,7 +203,7 @@ def tile_diffusionnetheatgradient_kernel(tc, s, lam, t, grad_bytes, grad_scale, 
         def finish(i):
             if not 0 <= i < UNITS:
                 return
-            o_sb = ring.tile([NP, C], F32, name="os")
+            o_sb = ring.tile([NP, C], F32, name="os", bufs=4)
             nc.scalar.activation(
                 out=o_sb[:].rearrange("v (c j) -> v c j", j=NT),
                 in_=ob[i][:].rearrange("v j c -> v c j"),
@@ -212,23 +218,28 @@ def tile_diffusionnetheatgradient_kernel(tc, s, lam, t, grad_bytes, grad_scale, 
             weights[name] = (codes, scales)
 
         with tc.manual_schedule():
-            load_chunk(0)
-            nc.sync.dma_start(out=s_raw[:], in_=s.rearrange("(p j) c -> p j c", j=NT))
-            nc.scalar.dma_start(out=t_row[:], in_=t.partition_broadcast(NP))
+            nc.vector.memset(t_rows[:], 0.0)
+            nc.vector.memset(ones[:], 1.0)
             nc.scalar.dma_start(out=lam_col[:], in_=lam.rearrange("(p j) -> p j", j=NT))
+            nc.scalar.dma_start(out=t_rows[0:1, :], in_=t.rearrange("(o c) -> o c", o=1))
             nc.scalar.dma_start(out=scale_col[:], in_=grad_scale.rearrange("a b (p j) -> p (a b j)", j=NT))
             nc.scalar.dma_start(out=gain_col[:], in_=gain.rearrange("(p j) -> p j", j=NT))
+            load_chunk(0)
             load_chunk(1)
-            nc.sync.dma_start(out=ar_raw[:], in_=ar.rearrange("(p j) c -> p j c", j=NT))
+            load_chunk(2)
+            nc.sync.dma_start(out=s_raw[:], in_=s.rearrange("(p j) c -> p j c", j=NT))
             nc.sync.dma_start(out=ai_raw[:], in_=aim.rearrange("(p j) c -> p j c", j=NT))
-            for n in range(2, len(chunks)):
+            nc.sync.dma_start(out=ar_raw[:], in_=ar.rearrange("(p j) c -> p j c", j=NT))
+            for n in range(3, len(chunks)):
                 load_chunk(n)
 
             nc.vector.memset(warm[:], 0.0)
             nc.scalar.activation(out=warm_out[:], in_=warm[:], func=ACT.Exp)
             nc.vector.tensor_scalar(out=neg_lam[:], in0=lam_col[:], scalar1=-1.0, scalar2=None, op0=ALU.mult)
+            t_all = psum.tile([NP, C], F32, name="ob")
+            nc.tensor.matmul(out=t_all[:], lhsT=ones[:], rhs=t_rows[:], start=True, stop=True)
             for j in range(NT):
-                nc.scalar.activation(out=decay[:, j, :], in_=t_row[:], func=ACT.Exp, scale=neg_lam[:, j : j + 1])
+                nc.scalar.activation(out=decay[:, j, :], in_=t_all[:], func=ACT.Exp, scale=neg_lam[:, j : j + 1])
 
             h_grp = keep.tile([NP, NT * C], BF16, align_bytes=64)
             ar_grp = keep.tile([NP, NT * C], BF16, align_bytes=64)
@@ -241,47 +252,54 @@ def tile_diffusionnetheatgradient_kernel(tc, s, lam, t, grad_bytes, grad_scale, 
             def permuted(tile):
                 return tile[:].rearrange("p j (m t) -> p t m j", t=NT)
 
-            def prepare(name, raw_tile, grp, engine):
-                for tt in range(NT):
+            def prepare(raw_tile, grp, engine, tts, sign):
+                for tt in tts:
                     piece = grouped(grp)[:, tt, :, :]
                     source = permuted(raw_tile)[:, tt, :, :]
                     if engine == "scalar":
-                        nc.scalar.activation(out=piece, in_=source, func=ACT.Copy, scale=-1.0)
+                        nc.scalar.activation(out=piece, in_=source, func=ACT.Copy, scale=sign)
+                    elif engine == "vector":
+                        nc.vector.tensor_scalar(out=piece, in0=source, scalar1=sign, scalar2=None, op0=ALU.mult)
                     else:
-                        nc.gpsimd.tensor_scalar(out=piece, in0=source, scalar1=1.0, scalar2=0.0, op0=ALU.mult, op1=ALU.add)
+                        nc.gpsimd.tensor_scalar(out=piece, in0=source, scalar1=sign, scalar2=0.0, op0=ALU.mult, op1=ALU.add)
 
-            prepare("ar", ar_raw, ar_grp, "gpsimd")
-            prepare("ai", ai_raw, ai_grp, "gpsimd")
-            for step in range(-5, UNITS):
-                scale_x(step + 3)
-                if step == -3:
-                    nc.vector.tensor_tensor(out=grouped(h_grp), in0=permuted(decay), in1=permuted(s_raw), op=ALU.mult)
-                turn(step + 4)
-                cast(step + 5)
-                g_out(step + 2, 0)
-                g_out(step + 2, 1)
-                late = step + 1 == UNITS - 1
-                if not late:
-                    for part in range(2):
-                        product(step, part)
-                for p in range(P):
-                    gain_z(step + 1, p)
-                if late:
-                    quant_z(step + 1)
-                    for part in range(2):
-                        product(step, part)
-                    stage2(step + 1)
-                turn_back(step)
-                finish(step)
-                if step == -3:
-                    prepare("nai", ai_raw, nai_grp, "scalar")
+            for step in range(-5, UNITS + 1):
+                if step < UNITS - 1:
+                    quant(step)
+                if step == -2:
                     quant_weight("h", h_grp[:])
-                if step == -1:
+                if step == 0:
                     quant_weight("ar", ar_grp[:])
                     quant_weight("nai", nai_grp[:])
                     quant_weight("ai", ai_grp[:])
-                quant_x(step + 3)
-                if not late:
-                    quant_z(step + 1)
+                if step < UNITS - 1:
+                    stage2(step)
+                gain_z(step + 1, 0, nc.vector)
+                g_out(step + 1, 0)
+                gain_z(step + 1, 1, nc.gpsimd)
+                gain_z(step + 1, 0, nc.gpsimd)
+                gain_z(step + 1, 1, nc.vector)
+                if step == UNITS - 2:
+                    quant(step + 1)
                     stage2(step + 1)
-                stage1(step + 3)
+                stage1(step + 2)
+                if step == -1:
+                    prepare(ai_raw, nai_grp, "scalar", range(NT), -1.0)
+                cast(step + 5)
+                if step == -2:
+                    prepare(ar_raw, ar_grp, "scalar", range(NT), 1.0)
+                scale_x(step + 3)
+                g_out(step + 2, 1)
+                if step < UNITS - 2:
+                    turn_back(step - 2)
+                turn(step + 4)
+                if step < UNITS - 2:
+                    finish(step - 2)
+                for part in range(2):
+                    product(step - 1, part)
+                if step >= UNITS - 3:
+                    turn_back(step - 1)
+                    finish(step - 1)
+                if step == -3:
+                    nc.vector.tensor_tensor(out=grouped(h_grp), in0=permuted(decay), in1=permuted(s_raw), op=ALU.mult)
+                    prepare(ai_raw, ai_grp, "gpsimd", range(NT), 1.0)

@@ -18,8 +18,9 @@ ALU = mybir.AluOpType
 NP = 128
 NT = 4
 UNITS = V // NP
-V_CASTS = 3
-V_COLS = (128, 0)
+V_CASTS = 2
+V_COLS = (64, 0)
+SUM_T = 0
 W = P * NP * NT
 
 
@@ -180,15 +181,24 @@ def tile_diffusionnetheatgradient_kernel(tc, s, lam, t, grad_bytes, grad_scale, 
         def product(i, part):
             if not 0 <= i < UNITS:
                 return
-            prod = ring.tile([NP, NT, NP], F32, name="mm%d" % part, bufs=4)
+            prod = ring.tile([NP, NT, NP], F32, name="mm%d" % part, bufs=5)
             nc.vector.tensor_tensor(out=prod[:], in0=eb[i, part][:], in1=gs[i, part][:], op=ALU.mult)
             mm[i, part] = prod
+
+        def add_up(i):
+            if 0 <= i < UNITS and SUM_T > 0:
+                total = ring.tile([NP, SUM_T, NP], F32, name="total")
+                eng = nc.gpsimd if i < UNITS - 1 else nc.vector
+                eng.tensor_tensor(out=total[:], in0=mm[i, 0][:, 0:SUM_T, :], in1=mm[i, 1][:, 0:SUM_T, :], op=ALU.add)
+                mm[i, 2] = total
 
         def turn_back(i):
             if not 0 <= i < UNITS:
                 return
             bank = psum.tile([NP, NT, NP], F32, name="tb" if i in (UNITS - 4, UNITS - 2) else "ob")
-            for tt in range(NT):
+            for tt in range(SUM_T):
+                nc.tensor.transpose(bank[:, tt, :], mm[i, 2][:, tt, :], ident[:])
+            for tt in range(SUM_T, NT):
                 for part in range(2):
                     nc.tensor.matmul(
                         out=bank[:, tt, :],
@@ -223,13 +233,13 @@ def tile_diffusionnetheatgradient_kernel(tc, s, lam, t, grad_bytes, grad_scale, 
             nc.scalar.dma_start(out=lam_col[:], in_=lam.rearrange("(p j) -> p j", j=NT))
             nc.scalar.dma_start(out=t_rows[0:1, :], in_=t.rearrange("(o c) -> o c", o=1))
             nc.scalar.dma_start(out=scale_col[:], in_=grad_scale.rearrange("a b (p j) -> p (a b j)", j=NT))
-            nc.scalar.dma_start(out=gain_col[:], in_=gain.rearrange("(p j) -> p j", j=NT))
             load_chunk(0)
             load_chunk(1)
-            load_chunk(2)
             nc.sync.dma_start(out=s_raw[:], in_=s.rearrange("(p j) c -> p j c", j=NT))
             nc.sync.dma_start(out=ai_raw[:], in_=aim.rearrange("(p j) c -> p j c", j=NT))
+            load_chunk(2)
             nc.sync.dma_start(out=ar_raw[:], in_=ar.rearrange("(p j) c -> p j c", j=NT))
+            nc.sync.dma_start(out=gain_col[:], in_=gain.rearrange("(p j) -> p j", j=NT))
             for n in range(3, len(chunks)):
                 load_chunk(n)
 
@@ -277,6 +287,8 @@ def tile_diffusionnetheatgradient_kernel(tc, s, lam, t, grad_bytes, grad_scale, 
                 gain_z(step + 1, 0, nc.vector)
                 g_out(step + 1, 0)
                 gain_z(step + 1, 1, nc.gpsimd)
+                if step < UNITS - 2:
+                    add_up(step - 2)
                 gain_z(step + 1, 0, nc.gpsimd)
                 gain_z(step + 1, 1, nc.vector)
                 if step == UNITS - 2:
@@ -290,14 +302,14 @@ def tile_diffusionnetheatgradient_kernel(tc, s, lam, t, grad_bytes, grad_scale, 
                     prepare(ar_raw, ar_grp, "scalar", range(NT), 1.0)
                 scale_x(step + 3)
                 g_out(step + 2, 1)
-                if step < UNITS - 2:
-                    turn_back(step - 2)
                 turn(step + 4)
                 if step < UNITS - 2:
+                    turn_back(step - 2)
                     finish(step - 2)
                 for part in range(2):
                     product(step - 1, part)
                 if step >= UNITS - 3:
+                    add_up(step - 1)
                     turn_back(step - 1)
                     finish(step - 1)
                 if step == -3:

from contextlib import ExitStack

import concourse.mybir as mybir
from concourse.masks import make_identity

V, M, C, P = 2048, 512, 512, 2
FLOPS = 2 * P * V * M * C + 4 * 2 * V * C * C

F32 = mybir.dt.float32
BF16 = mybir.dt.bfloat16
U32 = mybir.dt.uint32
U8 = mybir.dt.uint8
FP8 = mybir.dt.float8_e4m3fn
FP8X4 = mybir.dt.float8_e4m3fn_x4
ACT = mybir.ActivationFunctionType
ALU = mybir.AluOpType

NP = 128
NT = 4
UNITS = V // NP
V_CASTS = 2
V_COLS = (64, 0)
SUM_T = 0
W = P * NP * NT


def tile_diffusionnetheatgradient_kernel(tc, s, lam, t, grad_bytes, grad_scale, gain, ar, aim, out):
    nc = tc.nc
    with ExitStack() as ctx:
        keep = ctx.enter_context(tc.tile_pool(name="keep", bufs=1))
        ring = ctx.enter_context(tc.tile_pool(name="ring", bufs=3))
        psum = ctx.enter_context(tc.psum_pool(name="psum", bufs=1))

        ident = keep.tile([NP, NP], F32)
        make_identity(nc, ident[:])

        s_raw = keep.tile([NP, NT, C], BF16)
        ar_raw = keep.tile([NP, NT, C], BF16)
        ai_raw = keep.tile([NP, NT, C], BF16)
        t_rows = keep.tile([NP, C], BF16)
        ones = keep.tile([NP, NP], BF16)
        lam_col = keep.tile([NP, NT], BF16)
        neg_lam = keep.tile([NP, NT], F32)
        gain_col = keep.tile([NP, NT], BF16)
        scale_col = keep.tile([NP, NT], F32)
        decay = keep.tile([NP, NT, C], F32)
        warm = keep.tile([NP, 1], F32)
        warm_out = keep.tile([NP, 1], F32)

        raw = {}
        chunks = [(0, 1), (1, 1), (2, 2), (4, 4), (8, 4), (12, 4)]
        by_unit = {}

        def load_chunk(n):
            first, count = chunks[n]
            codes = keep.tile([NP, count, P, M], U8, name="bytes%d" % n)
            view = grad_bytes.rearrange("p (q i) k -> q i p k", i=UNITS)
            for i in range(count):
                nc.sync.dma_start(out=codes[:, i, :, :], in_=view[:, first + i, :, :])
            for i in range(count):
                by_unit[first + i] = codes[:, i, :, :]

        xb, tb, xc, gb, gs, zc, eb, mm, ob, pairs = {}, {}, {}, {}, {}, {}, {}, {}, {}, {}
        weights = {}

        def cast(i):
            if not 0 <= i < UNITS:
                return
            x_bf = ring.tile([NP, P * M], BF16)
            codes = by_unit[i].rearrange("q p k -> q (p k)").bitcast(FP8)
            if i < V_CASTS:
                nc.vector.tensor_copy(out=x_bf[:], in_=codes)
            else:
                nc.scalar.copy(out=x_bf[:], in_=codes)
            xb[i] = x_bf

        def turn(i):
            if not 0 <= i < UNITS:
                return
            bank = psum.tile([NP, 2, P * NP], F32, name="tb")
            words = xb[i][:].bitcast(F32)
            for p in range(P):
                for u in range(2):
                    nc.tensor.transpose(
                        bank[:, u, p * NP : (p + 1) * NP],
                        words[:, p * 256 + u : (p + 1) * 256 : 2],
                        ident[:],
                    )
            tb[i] = bank

        def scale_x(i):
            if not 0 <= i < UNITS:
                return
            nc.vector.tensor_tensor(
                out=pair_tile(i - 2)[:, 0:W].rearrange("k (r u e) -> k r u e", u=2, e=2),
                in0=tb[i][:].rearrange("k u r -> k (u r)").bitcast(BF16).rearrange("k (u r e) -> k r u e", u=2, e=2),
                in1=scale_col[:].rearrange("k (u e) -> k u e", u=2).unsqueeze(1).to_broadcast([NP, P * NP, 2, 2]),
                op=ALU.mult,
            )

        def pair_tile(n):
            if n not in pairs:
                pair = keep.tile([NP, 2 * W], BF16, align_bytes=64)
                pairs[n] = pair
            return pairs[n]

        def quant(n):
            has_x, has_z = 0 <= n + 2 < UNITS, 0 <= n < UNITS
            if not (has_x or has_z):
                return
            lo, hi = (0 if has_x else W), (2 * W if has_z else W)
            codes = ring.tile([NP, 2 * W // NT], U32, align_bytes=64)
            scales = ring.tile([NP, 2 * W // NT], U8, align_bytes=64)
            nc.vector.quantize_mx(
                out=codes[:, lo // NT : hi // NT].bitcast(FP8X4),
                scales=scales[:, lo // NT : hi // NT],
                in_=pairs[n][:, lo:hi],
            )
            if has_x:
                xc[n + 2] = (codes, scales, 0)
            if has_z:
                zc[n] = (codes, scales, W // NT)

        def mx(dst, w, tt, mov, p, start, stop):
            wc, ws = weights[w]
            cols = slice(tt * NP, (tt + 1) * NP)
            rows = slice(mov[2] + p * NP, mov[2] + (p + 1) * NP)
            nc.tensor.matmul_mx(
                out=dst,
                lhsT=wc[:, cols].bitcast(FP8X4),
                lhsT_scale=ws[:, cols],
                rhs=mov[0][:, rows].bitcast(FP8X4),
                rhs_scale=mov[1][:, rows],
                start=start,
                stop=stop,
            )

        def stage1(i):
            if not 0 <= i < UNITS:
                return
            for p in (1, 0):
                bank = psum.tile([NP, NT, NP], F32, name="gb%d" % p)
                for tt in range(NT):
                    mx(bank[:, tt, :], "h", tt, xc[i], p, True, True)
                gb[i, p] = bank

        def g_out(i, p):
            if not 0 <= i < UNITS:
                return
            g_sb = ring.tile([NP, NT, NP], F32, name="gs%d" % p, bufs=4)
            nc.scalar.copy(out=g_sb[:], in_=gb[i, p][:])
            gs[i, p] = g_sb

        def gain_z(i, p, eng):
            if not 0 <= i < UNITS:
                return
            cut = NP if i == UNITS - 1 else V_COLS[p]
            lo, hi, g_in = (0, cut, gb[i, p]) if eng is nc.vector else (cut, NP, gs.get((i, p)))
            if lo < hi:
                start = W + p * W // 2
                eng.tensor_tensor(
                    out=pair_tile(i)[:, start + lo * NT : start + hi * NT].rearrange("c (n j) -> c n j", j=NT),
                    in0=g_in[:, :, lo:hi].rearrange("c j n -> c n j"),
                    in1=gain_col[:].unsqueeze(1).to_broadcast([NP, hi - lo, NT]),
                    op=ALU.mult,
                )

        def stage2(i):
            if not 0 <= i < UNITS:
                return
            for part, w0, w1 in ((0, "ar", "nai"), (1, "ai", "ar")):
                if i == UNITS - 1:
                    bank = psum.tile([NP, NT, NP], F32, name="gb%d" % part)
                else:
                    bank = psum.tile([NP, NT, NP], F32, name="eb%d" % part, bufs=2)
                for tt in range(NT):
                    mx(bank[:, tt, :], w0, tt, zc[i], 0, True, False)
                    mx(bank[:, tt, :], w1, tt, zc[i], 1, False, True)
                eb[i, part] = bank

        def product(i, part):
            if not 0 <= i < UNITS:
                return
            prod = ring.tile([NP, NT, NP], F32, name="mm%d" % part, bufs=5)
            nc.vector.tensor_tensor(out=prod[:], in0=eb[i, part][:], in1=gs[i, part][:], op=ALU.mult)
            mm[i, part] = prod

        def add_up(i):
            if 0 <= i < UNITS and SUM_T > 0:
                total = ring.tile([NP, SUM_T, NP], F32, name="total")
                eng = nc.gpsimd if i < UNITS - 1 else nc.vector
                eng.tensor_tensor(out=total[:], in0=mm[i, 0][:, 0:SUM_T, :], in1=mm[i, 1][:, 0:SUM_T, :], op=ALU.add)
                mm[i, 2] = total

        def turn_back(i):
            if not 0 <= i < UNITS:
                return
            bank = psum.tile([NP, NT, NP], F32, name="tb" if i in (UNITS - 4, UNITS - 2) else "ob")
            for tt in range(SUM_T):
                nc.tensor.transpose(bank[:, tt, :], mm[i, 2][:, tt, :], ident[:])
            for tt in range(SUM_T, NT):
                for part in range(2):
                    nc.tensor.matmul(
                        out=bank[:, tt, :],
                        lhsT=mm[i, part][:, tt, :],
                        rhs=ident[:],
                        is_transpose=True,
                        start=(part == 0),
                        stop=(part == 1),
                    )
            ob[i] = bank

        def finish(i):
            if not 0 <= i < UNITS:
                return
            o_sb = ring.tile([NP, C], F32, name="os", bufs=4)
            nc.scalar.activation(
                out=o_sb[:].rearrange("v (c j) -> v c j", j=NT),
                in_=ob[i][:].rearrange("v j c -> v c j"),
                func=ACT.Tanh,
            )
            nc.sync.dma_start(out=out.rearrange("(q i) c -> q i c", i=UNITS)[:, i, :], in_=o_sb[:])

        def quant_weight(name, src):
            codes = keep.tile([NP, C], U32, align_bytes=64, name=name + "_c")
            scales = keep.tile([NP, C], U8, align_bytes=64, name=name + "_s")
            nc.vector.quantize_mx(out=codes[:].bitcast(FP8X4), scales=scales[:], in_=src)
            weights[name] = (codes, scales)

        with tc.manual_schedule():
            nc.vector.memset(t_rows[:], 0.0)
            nc.vector.memset(ones[:], 1.0)
            nc.scalar.dma_start(out=lam_col[:], in_=lam.rearrange("(p j) -> p j", j=NT))
            nc.scalar.dma_start(out=t_rows[0:1, :], in_=t.rearrange("(o c) -> o c", o=1))
            nc.scalar.dma_start(out=scale_col[:], in_=grad_scale.rearrange("a b (p j) -> p (a b j)", j=NT))
            load_chunk(0)
            load_chunk(1)
            nc.sync.dma_start(out=s_raw[:], in_=s.rearrange("(p j) c -> p j c", j=NT))
            nc.sync.dma_start(out=ai_raw[:], in_=aim.rearrange("(p j) c -> p j c", j=NT))
            load_chunk(2)
            nc.sync.dma_start(out=ar_raw[:], in_=ar.rearrange("(p j) c -> p j c", j=NT))
            nc.sync.dma_start(out=gain_col[:], in_=gain.rearrange("(p j) -> p j", j=NT))
            for n in range(3, len(chunks)):
                load_chunk(n)

            nc.vector.memset(warm[:], 0.0)
            nc.scalar.activation(out=warm_out[:], in_=warm[:], func=ACT.Exp)
            nc.vector.tensor_scalar(out=neg_lam[:], in0=lam_col[:], scalar1=-1.0, scalar2=None, op0=ALU.mult)
            t_all = psum.tile([NP, C], F32, name="ob")
            nc.tensor.matmul(out=t_all[:], lhsT=ones[:], rhs=t_rows[:], start=True, stop=True)
            for j in range(NT):
                nc.scalar.activation(out=decay[:, j, :], in_=t_all[:], func=ACT.Exp, scale=neg_lam[:, j : j + 1])

            h_grp = keep.tile([NP, NT * C], BF16, align_bytes=64)
            ar_grp = keep.tile([NP, NT * C], BF16, align_bytes=64)
            ai_grp = keep.tile([NP, NT * C], BF16, align_bytes=64)
            nai_grp = keep.tile([NP, NT * C], BF16, align_bytes=64)

            def grouped(tile):
                return tile[:].rearrange("p (t m j) -> p t m j", t=NT, j=NT)

            def permuted(tile):
                return tile[:].rearrange("p j (m t) -> p t m j", t=NT)

            def prepare(raw_tile, grp, engine, tts, sign):
                for tt in tts:
                    piece = grouped(grp)[:, tt, :, :]
                    source = permuted(raw_tile)[:, tt, :, :]
                    if engine == "scalar":
                        nc.scalar.activation(out=piece, in_=source, func=ACT.Copy, scale=sign)
                    elif engine == "vector":
                        nc.vector.tensor_scalar(out=piece, in0=source, scalar1=sign, scalar2=None, op0=ALU.mult)
                    else:
                        nc.gpsimd.tensor_scalar(out=piece, in0=source, scalar1=sign, scalar2=0.0, op0=ALU.mult, op1=ALU.add)

            for step in range(-5, UNITS + 1):
                if step < UNITS - 1:
                    quant(step)
                if step == -2:
                    quant_weight("h", h_grp[:])
                if step == 0:
                    quant_weight("ar", ar_grp[:])
                    quant_weight("nai", nai_grp[:])
                    quant_weight("ai", ai_grp[:])
                if step < UNITS - 1:
                    stage2(step)
                gain_z(step + 1, 0, nc.vector)
                g_out(step + 1, 0)
                gain_z(step + 1, 1, nc.gpsimd)
                if step < UNITS - 2:
                    add_up(step - 2)
                gain_z(step + 1, 0, nc.gpsimd)
                gain_z(step + 1, 1, nc.vector)
                if step == UNITS - 2:
                    quant(step + 1)
                    stage2(step + 1)
                stage1(step + 2)
                if step == -1:
                    prepare(ai_raw, nai_grp, "scalar", range(NT), -1.0)
                cast(step + 5)
                if step == -2:
                    prepare(ar_raw, ar_grp, "scalar", range(NT), 1.0)
                scale_x(step + 3)
                g_out(step + 2, 1)
                turn(step + 4)
                if step < UNITS - 2:
                    turn_back(step - 2)
                    finish(step - 2)
                for part in range(2):
                    product(step - 1, part)
                if step >= UNITS - 3:
                    add_up(step - 1)
                    turn_back(step - 1)
                    finish(step - 1)
                if step == -3:
                    nc.vector.tensor_tensor(out=grouped(h_grp), in0=permuted(decay), in1=permuted(s_raw), op=ALU.mult)
                    prepare(ai_raw, ai_grp, "gpsimd", range(NT), 1.0)
